import numpy as np
import ml_dtypes


def mxq(x, axis, fmt="e4m3"):
    dtype, down = {"e4m3": (ml_dtypes.float8_e4m3fn, 7), "e5m2": (ml_dtypes.float8_e5m2, 14)}[fmt]
    v = np.moveaxis(np.asarray(x, np.float32).astype(ml_dtypes.bfloat16).astype(np.float64), axis, -1)
    blocks = v.reshape(v.shape[:-1] + (-1, 32))
    amax = np.abs(blocks).max(-1, keepdims=True)
    byte = np.maximum(np.where(amax > 0, np.frexp(amax)[1] - 1 + 127, 0) - down, 1)
    scale = np.exp2(byte - 127.0)
    codes = (blocks / scale).astype(np.float32).astype(dtype).astype(np.float64)
    return np.moveaxis((codes * scale).reshape(v.shape), -1, axis)


WIDE = False


def mx_kscale(k):
    if not WIDE:
        return np.ones(k)
    levels = np.array([10, -10, 5, -5, 0])
    if k % 512:
        return np.exp2(np.random.permutation(np.resize(levels, k // 32))).repeat(32)
    a = np.empty((k // 512, 16))
    for p in range(k // 512):
        a[p, :8] = np.random.permutation(np.resize(levels, 8))
        for g in range(8):
            far = levels[np.abs(levels - a[p, g]) >= 10]
            a[p, g + 8] = far[np.random.randint(len(far))]
    return np.exp2(a.ravel()).repeat(32)


def f64(x):
    return np.asarray(x).astype(np.float64)


def striped(idx):
    return np.tile(idx.reshape(-1, 16).T, (8, 1)).astype(np.uint16)


def unstriped(offs):
    return offs[:16].T.reshape(-1).astype(np.int64)


E2M1 = np.array([0.0, 0.5, 1.0, 1.5, 2.0, 3.0, 4.0, 6.0, -0.0, -0.5, -1.0, -1.5, -2.0, -3.0, -4.0, -6.0])


def pack_weight(w, fmt):
    k, n = w.shape
    w = f64(np.asarray(w, np.float32).astype(ml_dtypes.bfloat16)).reshape(k // 32, 32, n)
    amax = np.abs(w).max(1)
    if fmt == "e4m3":
        byte = np.frexp(amax)[1] - 1 + 127 - 7
    else:
        mant, ex = np.frexp(amax / 6.0)
        byte = np.where(mant > 0.5, ex, ex - 1) + 127
    byte = np.clip(np.where(amax > 0, byte, 1), 1, 254)
    scaled = (w * np.exp2(127.0 - byte)[:, None, :]).reshape(k, n).astype(np.float32)
    by_word = np.ascontiguousarray(scaled.reshape(k // 512, 128, 4, n).transpose(0, 1, 3, 2))
    if fmt == "e4m3":
        words = by_word.astype(ml_dtypes.float8_e4m3fn).view(np.uint8)
    else:
        c = by_word.astype(ml_dtypes.float4_e2m1fn).view(np.uint8) & 0xF
        words = (c[..., 0::2] | (c[..., 1::2] << 4)).reshape(k // 512, 128, 2 * n)
    return np.ascontiguousarray(words), np.ascontiguousarray(byte.astype(np.uint8).reshape(k // 512, 16, n))


def unpack_weight(words, scales, fmt):
    g, _, n = scales.shape
    words = np.ascontiguousarray(words).reshape(g, 128, n, -1)
    if fmt == "e4m3":
        vals = words.view(ml_dtypes.float8_e4m3fn).astype(np.float64)
    else:
        nib = np.empty((g, 128, n, 4), np.uint8)
        nib[..., 0::2] = words & 0xF
        nib[..., 1::2] = words >> 4
        vals = E2M1[nib]
    vals = vals * np.repeat(np.exp2(scales.astype(np.float64) - 127.0), 8, axis=1)[..., None]
    return vals.transpose(0, 1, 3, 2).reshape(g * 512, n)


def relu(v):
    return np.maximum(v, 0.0)


K, T, E, C, H, N = 512, 512, 8, 256, 512, 384
TOP = 4


def by_expert(wq, xq):
    return np.concatenate([wq[e].T @ xq[:, e * C:(e + 1) * C] for e in range(E)], axis=1)


def setup_inputs():
    n = np.random.standard_normal
    s = mx_kscale(K)[:, None]
    u = mx_kscale(H)
    deal = np.repeat(np.arange(E), C).reshape(TOP, T)[:, np.random.permutation(T)]
    deal = np.take_along_axis(deal, np.argsort(np.random.rand(TOP, T), axis=0), axis=0)
    for _ in range(8):
        s_, t_ = np.random.permutation(T).reshape(2, -1); r = np.random.randint(TOP, size=T // 2); x, y = deal[r, s_].copy(), deal[r, t_].copy()
        ok = ~((deal[:, s_] == y).any(0) | (deal[:, t_] == x).any(0)); deal[r[ok], s_[ok]] = y[ok]; deal[r[ok], t_[ok]] = x[ok]
    order = np.lexsort((np.random.rand(TOP * T), deal.reshape(-1)))
    slot_token = order % T; pos = np.empty(TOP * T, np.int64); pos[order] = np.arange(TOP * T); pos = pos.reshape(TOP, T)
    g = np.random.uniform(0.5, 1.5, (TOP, T)); g = g / g.sum(0)
    w1 = [pack_weight(m, "e2m1") for m in n((E + 1, K, H)) / np.sqrt(K) / s[None] * u[None, None, :]]
    w2 = [pack_weight(m, "e2m1") for m in n((E + 1, H, N)) / np.sqrt(H) / u[None, :, None]]
    return {
        "xT": (n((K, T)) * s).astype(np.float32),
        "w1_words": np.stack([m[0] for m in w1]),
        "w1_scales": np.stack([m[1] for m in w1]),
        "w2_words": np.stack([m[0] for m in w2]),
        "w2_scales": np.stack([m[1] for m in w2]),
        "gate": np.stack([np.tile(r, (N, 1)) for r in g]).astype(np.float32),
        "offs": striped(slot_token),
        "pos1": striped(pos[0]),
        "pos2": striped(pos[1]),
        "pos3": striped(pos[2]),
        "pos4": striped(pos[3]),
    }


def reference(xT, w1_words, w1_scales, w2_words, w2_scales, gate, offs, pos1, pos2, pos3, pos4):
    idx = unstriped(offs)
    w1 = np.stack([unpack_weight(w1_words[e], w1_scales[e], "e2m1") for e in range(E + 1)])
    w2 = np.stack([unpack_weight(w2_words[e], w2_scales[e], "e2m1") for e in range(E + 1)])
    w1q, w2q = w1, w2
    xs = mxq(f64(xT), 0, "e4m3")
    hs = relu(w1q[E].T @ xs)
    ys = w2q[E].T @ mxq(hs, 0, "e4m3")
    xq = mxq(f64(xT)[:, idx], 0, "e4m3")
    h = relu(by_expert(w1q, xq))
    y = by_expert(w2q, mxq(h, 0, "e4m3"))
    return ys + sum(f64(gate[r]) * y[:, unstriped(p)] for r, p in enumerate((pos1, pos2, pos3, pos4)))

@@ -1,0 +1,264 @@
+from contextlib import ExitStack
+
+import concourse.mybir as mybir
+from concourse.masks import make_identity
+
+K, T, E, C, H, N = 512, 512, 8, 256, 512, 384
+TOP = 4
+S = E * C
+FLOPS = 2 * (S + T) * (K * H + H * N)
+BYTES = 4 * K * T + (E + 1) * (K * H + H * N) // 2 + (E + 1) * (K * H + H * N) // 32 + 4 * TOP * T + 4 * N * T
+
+F32 = mybir.dt.float32
+BF16 = mybir.dt.bfloat16
+I32 = mybir.dt.int32
+U32 = mybir.dt.uint32
+U16 = mybir.dt.uint16
+U8 = mybir.dt.uint8
+FP8X4 = mybir.dt.float8_e4m3fn_x4
+FP4X4 = mybir.dt.float4_e2m1fn_x4
+RELU = mybir.ActivationFunctionType.Relu
+MULT = mybir.AluOpType.mult
+ADD = mybir.AluOpType.add
+
+P = 128
+PACK = 4
+NB = N // P
+PSUM_BUFS = {"wide": 3, "first": 2, "later": 2, "turned": 1}
+W1_GROUPS = ((0, 4), (4, 9))
+
+
+def tile_moe_shr_mlp_relu_kernel(
+    tc, xT, w1_words, w1_scales, w2_words, w2_scales, gate, offs, pos1, pos2, pos3, pos4, out
+):
+    nc = tc.nc
+    with ExitStack() as ctx:
+        keep = ctx.enter_context(tc.tile_pool(name="keep", bufs=1))
+        ring = ctx.enter_context(tc.tile_pool(name="ring", bufs=2))
+        psum = ctx.enter_context(tc.psum_pool(name="psum", bufs=1))
+
+        def bank(shape, tag):
+            return psum.tile(shape, F32, name=tag, bufs=PSUM_BUFS[tag])
+
+        s1_raw = [keep.tile([P, e1 - e0, H], U8, name="s1_raw%d" % e0, align_bytes=64) for e0, e1 in W1_GROUPS]
+        nc.gpsimd.memset(s1_raw[0][:].bitcast(I32), 0)
+        ident_raw = keep.tile([P, P], F32, name="ident_raw")
+        make_identity(nc, ident_raw[:])
+        ident = keep.tile([P, P], F32, name="ident")
+        nc.scalar.activation(ident[:], ident_raw[:], RELU)
+
+        s2 = keep.tile([P, E + 1, N], U8, name="s2", align_bytes=64)
+        nc.vector.memset(s1_raw[1][:].bitcast(I32), 0)
+        nc.vector.memset(s2[:].bitcast(I32), 0)
+
+        def load_words(words, e0, e1, name, tag):
+            t = keep.tile([P, e1 - e0, words.shape[3]], U8, name=name, tag=tag, align_bytes=64)
+            nc.sync.dma_start(t[:].bitcast(I32), words[e0:e1, 0].rearrange("e p b -> p e b").bitcast(I32))
+            return t
+
+        def load_scales(plane, scales):
+            rows = scales[:, 0].rearrange("e (q r) b -> r q e b", r=4)
+            for r in range(4):
+                nc.sync.dma_start(plane[r:P:32, :, :].bitcast(I32), rows[r].bitcast(I32))
+
+        def load_list(lst, name):
+            t = keep.tile([P, lst.shape[1]], U16, name=name)
+            nc.sync.dma_start(t[:], lst)
+            return t
+
+        x_rows = xT.rearrange("(p u j) t -> u p j t", u=2, j=2)
+        w1_raw = [load_words(w1_words, 0, 4, "w1_raw0", "w1_raw0")]
+        x_raw = []
+        for u in range(2):
+            t = keep.tile([P, 2, T], F32, name="x_raw%d" % u, tag="x_raw%d" % u, align_bytes=64)
+            nc.sync.dma_start(t[:], x_rows[u])
+            x_raw.append(t)
+        load_scales(s1_raw[0], w1_scales[0:4])
+        offs_sb = load_list(offs, "offs_sb")
+        pos_sb = [load_list(lst, "pos_sb%d" % r) for r, lst in enumerate((pos1, pos2, pos3, pos4))]
+        load_scales(s1_raw[1], w1_scales[4:9])
+
+        pairs = keep.tile([P, 2 * T], U32, name="pairs", tag="pairs", align_bytes=64)
+        for u in range(2):
+            nc.scalar.copy(
+                pairs[:, u * T : (u + 1) * T].bitcast(BF16).rearrange("p (t j) -> p t j", j=2),
+                x_raw[u][:].rearrange("p j t -> p t j"),
+            )
+
+        w1_raw.append(load_words(w1_words, 4, 9, "w1_raw1", "x_raw0"))
+        w2 = load_words(w2_words, 0, E + 1, "w2", "x_raw1")
+        load_scales(s2, w2_scales)
+
+        w1 = {}
+        s1 = {}
+
+        def permute(e):
+            g = 0 if e < 4 else 1
+            src = w1_raw[g][:, e - W1_GROUPS[g][0], :].bitcast(U16)
+            if e == E:
+                w1[e] = keep.tile([P, 2 * H], U8, name="w1_shared", tag="hg6", align_bytes=64)
+            else:
+                w1[e] = ring.tile([P, 2 * H], U8, name="w1", align_bytes=64, bufs=4)
+            nc.vector.tensor_copy(
+                w1[e][:].bitcast(U16).rearrange("p (t a b) -> p a t b", t=PACK, b=8),
+                src.rearrange("p (a b t) -> p a t b", t=PACK, b=8),
+            )
+            s1[e] = ring.tile([P, H], U8, name="s1", align_bytes=64, bufs=4)
+            nc.vector.tensor_copy(
+                s1[e][:].rearrange("p (t a b) -> p a t b", t=PACK, b=16),
+                s1_raw[g][:, e - W1_GROUPS[g][0], :].rearrange("p (a b t) -> p a t b", t=PACK, b=16),
+            )
+
+        def quantize(grouped, width, name, tag):
+            codes = keep.tile([P, width], U32, name=name + "_codes", tag=tag, align_bytes=64)
+            scales = keep.tile([P, width], U8, name=name + "_scales", align_bytes=64)
+            nc.vector.quantize_mx(out=codes[:].bitcast(FP8X4), scales=scales[:], in_=grouped)
+            return codes, scales
+
+        picked = {}
+        xg = {}
+        xq = {}
+        hg = {}
+        hq = {}
+
+        def gather_tokens(e):
+            picked[e] = keep.tile([P, 2, C], U32, name="picked%d" % e, tag="slot%d" % (e % 3), align_bytes=64)
+            for u in range(2):
+                nc.vector.tensor_copy(picked[e][:, u, :], pairs[:, u * T : (u + 1) * T].indirect(offs_sb[:, 16 * e : 16 * (e + 1)]))
+
+        def weave(e):
+            xg[e] = keep.tile([P, C, 2], U32, name="xg%d" % e, tag="slot%d" % ((e + 2) % 3), align_bytes=64)
+            nc.scalar.copy(xg[e][:], picked[e][:].rearrange("p u c -> p c u"))
+
+        def quantize_x(e):
+            width = T if e == E else C
+            xq[e] = quantize(xg[e][:].rearrange("p c u -> p (c u)").bitcast(BF16), width, "xq%d" % e, "hg7" if e == E else "xq%d" % e)
+
+        def layer1(e):
+            width = T if e == E else C
+            codes, scales = xq[e]
+            hg[e] = keep.tile([P, width, PACK], BF16, name="hg%d" % e, tag="hg%d" % e, align_bytes=64)
+            for c0 in range(0, width, P):
+                a = bank([P, PACK, P], "wide")
+                for t in range(PACK):
+                    nc.tensor.matmul_mx(
+                        out=a[:, t, :],
+                        lhsT=w1[e][:, 2 * P * t : 2 * P * (t + 1)].bitcast(FP4X4),
+                        lhsT_scale=s1[e][:, P * t : P * (t + 1)],
+                        rhs=codes[:, c0 : c0 + P].bitcast(FP8X4),
+                        rhs_scale=scales[:, c0 : c0 + P],
+                        start=True,
+                        stop=True,
+                    )
+                nc.scalar.activation(hg[e][:, c0 : c0 + P, :], a[:].rearrange("p t c -> p c t"), RELU)
+
+        def quantize_h(e):
+            width = T if e == E else C
+            hq[e] = quantize(hg[e][:].rearrange("p c t -> p (c t)"), width, "hq%d" % e, "hq%d" % e)
+
+        def layer2(e, b, dst):
+            codes, scales = hq[e]
+            nc.tensor.matmul_mx(
+                out=dst,
+                lhsT=w2[:, e, 2 * P * b : 2 * P * (b + 1)].bitcast(FP4X4),
+                lhsT_scale=s2[:, e, P * b : P * (b + 1)],
+                rhs=codes[:].bitcast(FP8X4),
+                rhs_scale=scales[:],
+                start=True,
+                stop=True,
+            )
+
+        y = {0: keep.tile([P, S], F32, name="y0")}
+        ys = [keep.tile([P, T], F32, name="ys%d" % b) for b in range(NB)]
+
+        def slots_results(b, e0, e1):
+            acc = bank([P, (e1 - e0) * C], "first" if b == 0 else "later")
+            for e in range(e0, e1):
+                layer2(e, b, acc[:, (e - e0) * C : (e - e0 + 1) * C])
+            nc.scalar.copy(y[b][:, e0 * C : e1 * C], acc[:])
+
+        def shared_results(b):
+            acc = bank([P, T], "later")
+            layer2(E, b, acc[:])
+            nc.scalar.copy(ys[b][:], acc[:])
+
+        xg[E] = keep.tile([P, T, 2], U32, name="xg_shared", align_bytes=64)
+        nc.scalar.copy(xg[E][:], pairs[:].rearrange("p (u t) -> p t u", u=2))
+
+
+        permute(0)
+        gather_tokens(0)
+        gather_tokens(1)
+        weave(0)
+        quantize_x(0)
+        layer1(0)
+        for e in range(E):
+            if e + 2 < E:
+                gather_tokens(e + 2)
+            if e + 1 < E:
+                permute(e + 1)
+                weave(e + 1)
+                quantize_x(e + 1)
+                layer1(e + 1)
+            if e == 2:
+                gate_sb = keep.tile([P, TOP, T], F32, name="gate_sb", tag="w1_raw0", align_bytes=64)
+                nc.sync.dma_start(gate_sb[:], gate[:, 0:P, :].rearrange("r p t -> p r t"))
+            quantize_h(e)
+            slots_results(0, e, e + 1)
+        permute(E)
+        quantize_x(E)
+
+        def product(b, r):
+            tag = "hg%d" % E if (b, r) == (0, TOP - 1) else "prod%d_%d" % (b, r)
+            prod = keep.tile([P, T], F32, name="prod", tag=tag, align_bytes=64)
+            nc.vector.tensor_tensor(prod[:], y[b][:].indirect(pos_sb[r][:]), gate_sb[:, r, :], MULT)
+            return prod
+
+        def add_up(terms):
+            turned = bank([P, T // P, P], "turned")
+            for i, term in enumerate(terms):
+                for j in range(T // P):
+                    nc.tensor.matmul(
+                        turned[:, j, :],
+                        term[:, j * P : (j + 1) * P],
+                        ident[:],
+                        start=(i == 0 and j == 0),
+                        stop=(i == len(terms) - 1 and j == T // P - 1),
+                        is_transpose=True,
+                    )
+            turned_sb = ring.tile([P, T // P, P], F32, name="turned_sb")
+            nc.scalar.copy(turned_sb[:], turned[:])
+            back = bank([P, T], "first")
+            for j in range(T // P):
+                nc.tensor.transpose(back[:, j * P : (j + 1) * P], turned_sb[:, j, :], ident[:])
+            return back
+
+        def store_sum(b, back):
+            result = ring.tile([P, T], F32, name="result")
+            nc.scalar.copy(result[:], back[:])
+            nc.sync.dma_start(out[b * P : (b + 1) * P, :], result[:])
+
+        prods0 = [product(0, r) for r in range(TOP - 1)]
+        layer1(E)
+        y[1] = keep.tile([P, S], F32, name="y1", tag="pairs", align_bytes=64)
+        for e0 in range(0, E, 2):
+            slots_results(1, e0, e0 + 2)
+        quantize_h(E)
+        prods0.append(product(0, TOP - 1))
+        prods1 = [product(1, r) for r in range(TOP)]
+        y[2] = keep.tile([P, S], F32, name="y2", tag="slot0", align_bytes=64)
+        for e0 in range(0, E, 2):
+            slots_results(2, e0, e0 + 2)
+        for b in range(NB):
+            shared_results(b)
+        store_sum(0, add_up(prods0 + [ys[0]]))
+        prods2 = [product(2, r) for r in range(TOP)]
+        store_sum(1, add_up([ys[1]] + prods1))
+        back = add_up([ys[2]] + prods2[:2])
+        partial = ring.tile([P, T], F32, name="partial")
+        nc.vector.tensor_tensor(partial[:], prods2[2][:], back[:], ADD)
+        for c0 in range(0, T, T // 2):
+            cols = slice(c0, c0 + T // 2)
+            result = ring.tile([P, T // 2], F32, name="last")
+            nc.vector.tensor_tensor(result[:], partial[:, cols], prods2[3][:, cols], ADD)
+            nc.sync.dma_start(out[2 * P : 3 * P, cols], result[:])

@@ -68,19 +68,20 @@ def tile_moe_shr_mlp_relu_kernel(
 
         x_rows = xT.rearrange("(p u j) t -> u p j t", u=2, j=2)
         w1_raw = [load_words(w1_words, 0, 4, "w1_raw0", "w1_raw0")]
+        load_scales(s1_raw[0], w1_scales[0:4])
         x_raw = []
         for u in range(2):
             t = keep.tile([P, 2, T], F32, name="x_raw%d" % u, tag="x_raw%d" % u, align_bytes=64)
             nc.sync.dma_start(t[:], x_rows[u])
             x_raw.append(t)
-        load_scales(s1_raw[0], w1_scales[0:4])
         offs_sb = load_list(offs, "offs_sb")
         pos_sb = [load_list(lst, "pos_sb%d" % r) for r, lst in enumerate((pos1, pos2, pos3, pos4))]
         load_scales(s1_raw[1], w1_scales[4:9])
 
         pairs = keep.tile([P, 2 * T], U32, name="pairs", tag="pairs", align_bytes=64)
         for u in range(2):
-            nc.scalar.copy(
+            cast = nc.scalar.copy if u == 0 else nc.vector.tensor_copy
+            cast(
                 pairs[:, u * T : (u + 1) * T].bitcast(BF16).rearrange("p (t j) -> p t j", j=2),
                 x_raw[u][:].rearrange("p j t -> p t j"),
             )
@@ -95,10 +96,7 @@ def tile_moe_shr_mlp_relu_kernel(
         def permute(e):
             g = 0 if e < 4 else 1
             src = w1_raw[g][:, e - W1_GROUPS[g][0], :].bitcast(U16)
-            if e == E:
-                w1[e] = keep.tile([P, 2 * H], U8, name="w1_shared", tag="hg6", align_bytes=64)
-            else:
-                w1[e] = ring.tile([P, 2 * H], U8, name="w1", align_bytes=64, bufs=4)
+            w1[e] = ring.tile([P, 2 * H], U8, name="w1", align_bytes=64, bufs=4)
             nc.vector.tensor_copy(
                 w1[e][:].bitcast(U16).rearrange("p (t a b) -> p a t b", t=PACK, b=8),
                 src.rearrange("p (a b t) -> p a t b", t=PACK, b=8),
@@ -128,7 +126,8 @@ def tile_moe_shr_mlp_relu_kernel(
 
         def weave(e):
             xg[e] = keep.tile([P, C, 2], U32, name="xg%d" % e, tag="slot%d" % ((e + 2) % 3), align_bytes=64)
-            nc.scalar.copy(xg[e][:], picked[e][:].rearrange("p u c -> p c u"))
+            move = nc.vector.tensor_copy if e == 0 else nc.scalar.copy
+            move(xg[e][:], picked[e][:].rearrange("p u c -> p c u"))
 
         def quantize_x(e):
             width = T if e == E else C
@@ -139,7 +138,7 @@ def tile_moe_shr_mlp_relu_kernel(
             codes, scales = xq[e]
             hg[e] = keep.tile([P, width, PACK], BF16, name="hg%d" % e, tag="hg%d" % e, align_bytes=64)
             for c0 in range(0, width, P):
-                a = bank([P, PACK, P], "wide")
+                a = bank([P, PACK, P], "first" if e == E else "wide")
                 for t in range(PACK):
                     nc.tensor.matmul_mx(
                         out=a[:, t, :],
@@ -154,7 +153,7 @@ def tile_moe_shr_mlp_relu_kernel(
 
         def quantize_h(e):
             width = T if e == E else C
-            hq[e] = quantize(hg[e][:].rearrange("p c t -> p (c t)"), width, "hq%d" % e, "hq%d" % e)
+            hq[e] = quantize(hg[e][:].rearrange("p c t -> p (c t)"), width, "hq%d" % e, "prod0_2" if e == E else "hq%d" % e)
 
         def layer2(e, b, dst):
             codes, scales = hq[e]
@@ -171,8 +170,8 @@ def tile_moe_shr_mlp_relu_kernel(
         y = {0: keep.tile([P, S], F32, name="y0")}
         ys = [keep.tile([P, T], F32, name="ys%d" % b) for b in range(NB)]
 
-        def slots_results(b, e0, e1):
-            acc = bank([P, (e1 - e0) * C], "first" if b == 0 else "later")
+        def slots_results(b, e0, e1, tag):
+            acc = bank([P, (e1 - e0) * C], tag)
             for e in range(e0, e1):
                 layer2(e, b, acc[:, (e - e0) * C : (e - e0 + 1) * C])
             nc.scalar.copy(y[b][:, e0 * C : e1 * C], acc[:])
@@ -204,31 +203,40 @@ def tile_moe_shr_mlp_relu_kernel(
                 gate_sb = keep.tile([P, TOP, T], F32, name="gate_sb", tag="w1_raw0", align_bytes=64)
                 nc.sync.dma_start(gate_sb[:], gate[:, 0:P, :].rearrange("r p t -> p r t"))
             quantize_h(e)
-            slots_results(0, e, e + 1)
+            if e >= 2 and e % 2 == 0:
+                slots_results(0, e - 2, e, "wide")
+            if e >= E - 2:
+                slots_results(0, e, e + 1, "first")
         permute(E)
         quantize_x(E)
 
         def product(b, r):
-            tag = "hg%d" % E if (b, r) == (0, TOP - 1) else "prod%d_%d" % (b, r)
+            tag = "hg%d" % E if (b, r) == (1, 0) else "prod%d_%d" % (b, r)
             prod = keep.tile([P, T], F32, name="prod", tag=tag, align_bytes=64)
             nc.vector.tensor_tensor(prod[:], y[b][:].indirect(pos_sb[r][:]), gate_sb[:, r, :], MULT)
             return prod
 
-        def add_up(terms):
-            turned = bank([P, T // P, P], "turned")
+        def turn(turned, terms, opens, closes):
             for i, term in enumerate(terms):
                 for j in range(T // P):
                     nc.tensor.matmul(
                         turned[:, j, :],
                         term[:, j * P : (j + 1) * P],
                         ident[:],
-                        start=(i == 0 and j == 0),
-                        stop=(i == len(terms) - 1 and j == T // P - 1),
+                        start=(opens and i == 0 and j == 0),
+                        stop=(closes and i == len(terms) - 1 and j == T // P - 1),
                         is_transpose=True,
                     )
+
+        def add_up(terms):
+            turned = bank([P, T // P, P], "turned")
+            turn(turned, terms, True, True)
+            return turn_back(turned)
+
+        def turn_back(turned):
             turned_sb = ring.tile([P, T // P, P], F32, name="turned_sb")
             nc.scalar.copy(turned_sb[:], turned[:])
-            back = bank([P, T], "first")
+            back = bank([P, T], "wide")
             for j in range(T // P):
                 nc.tensor.transpose(back[:, j * P : (j + 1) * P], turned_sb[:, j, :], ident[:])
             return back
@@ -238,27 +246,29 @@ def tile_moe_shr_mlp_relu_kernel(
             nc.scalar.copy(result[:], back[:])
             nc.sync.dma_start(out[b * P : (b + 1) * P, :], result[:])
 
-        prods0 = [product(0, r) for r in range(TOP - 1)]
+        prods0 = [product(0, r) for r in range(TOP)]
         layer1(E)
-        y[1] = keep.tile([P, S], F32, name="y1", tag="pairs", align_bytes=64)
+        y[1] = keep.tile([P, S], F32, name="y1", tag="hg6", align_bytes=64)
         for e0 in range(0, E, 2):
-            slots_results(1, e0, e0 + 2)
+            slots_results(1, e0, e0 + 2, "later" if e0 < E // 2 else "wide")
+        turned0 = bank([P, T // P, P], "turned")
+        turn(turned0, prods0, True, False)
         quantize_h(E)
-        prods0.append(product(0, TOP - 1))
         prods1 = [product(1, r) for r in range(TOP)]
-        y[2] = keep.tile([P, S], F32, name="y2", tag="slot0", align_bytes=64)
+        y[2] = keep.tile([P, S], F32, name="y2", tag="hg7", align_bytes=64)
         for e0 in range(0, E, 2):
-            slots_results(2, e0, e0 + 2)
+            slots_results(2, e0, e0 + 2, "later" if e0 < E // 2 else "wide")
         for b in range(NB):
             shared_results(b)
-        store_sum(0, add_up(prods0 + [ys[0]]))
+        turn(turned0, [ys[0]], False, True)
+        store_sum(0, turn_back(turned0))
         prods2 = [product(2, r) for r in range(TOP)]
         store_sum(1, add_up([ys[1]] + prods1))
         back = add_up([ys[2]] + prods2[:2])
         partial = ring.tile([P, T], F32, name="partial")
-        nc.vector.tensor_tensor(partial[:], prods2[2][:], back[:], ADD)
+        nc.vector.tensor_tensor(partial[:], prods2[2][:], prods2[3][:], ADD)
         for c0 in range(0, T, T // 2):
             cols = slice(c0, c0 + T // 2)
             result = ring.tile([P, T // 2], F32, name="last")
-            nc.vector.tensor_tensor(result[:], partial[:, cols], prods2[3][:, cols], ADD)
+            nc.vector.tensor_tensor(result[:], partial[:, cols], back[:, cols], ADD)
             nc.sync.dma_start(out[2 * P : 3 * P, cols], result[:])

@@ -80,8 +80,7 @@ def tile_moe_shr_mlp_relu_kernel(
 
         pairs = keep.tile([P, 2 * T], U32, name="pairs", tag="pairs", align_bytes=64)
         for u in range(2):
-            cast = nc.scalar.copy if u == 0 else nc.vector.tensor_copy
-            cast(
+            nc.scalar.copy(
                 pairs[:, u * T : (u + 1) * T].bitcast(BF16).rearrange("p (t j) -> p t j", j=2),
                 x_raw[u][:].rearrange("p j t -> p t j"),
             )
@@ -93,19 +92,22 @@ def tile_moe_shr_mlp_relu_kernel(
         w1 = {}
         s1 = {}
 
-        def permute(e):
-            g = 0 if e < 4 else 1
-            src = w1_raw[g][:, e - W1_GROUPS[g][0], :].bitcast(U16)
-            w1[e] = ring.tile([P, 2 * H], U8, name="w1", align_bytes=64, bufs=4)
+        def permute(e0, e1):
+            g = 0 if e0 < 4 else 1
+            held = slice(e0 - W1_GROUPS[g][0], e1 - W1_GROUPS[g][0])
+            words = ring.tile([P, e1 - e0, 2 * H], U8, name="w1", align_bytes=64, bufs=2)
             nc.vector.tensor_copy(
-                w1[e][:].bitcast(U16).rearrange("p (t a b) -> p a t b", t=PACK, b=8),
-                src.rearrange("p (a b t) -> p a t b", t=PACK, b=8),
+                words[:].bitcast(U16).rearrange("p e (t a b) -> p e a t b", t=PACK, b=8),
+                w1_raw[g][:, held, :].bitcast(U16).rearrange("p e (a b t) -> p e a t b", t=PACK, b=8),
             )
-            s1[e] = ring.tile([P, H], U8, name="s1", align_bytes=64, bufs=4)
+            scales = ring.tile([P, e1 - e0, H], U8, name="s1", align_bytes=64, bufs=2)
             nc.vector.tensor_copy(
-                s1[e][:].rearrange("p (t a b) -> p a t b", t=PACK, b=16),
-                s1_raw[g][:, e - W1_GROUPS[g][0], :].rearrange("p (a b t) -> p a t b", t=PACK, b=16),
+                scales[:].rearrange("p e (t a b) -> p e a t b", t=PACK, b=16),
+                s1_raw[g][:, held, :].rearrange("p e (a b t) -> p e a t b", t=PACK, b=16),
             )
+            for e in range(e0, e1):
+                w1[e] = words[:, e - e0, :]
+                s1[e] = scales[:, e - e0, :]
 
         def quantize(grouped, width, name, tag):
             codes = keep.tile([P, width], U32, name=name + "_codes", tag=tag, align_bytes=64)
@@ -126,8 +128,10 @@ def tile_moe_shr_mlp_relu_kernel(
 
         def weave(e):
             xg[e] = keep.tile([P, C, 2], U32, name="xg%d" % e, tag="slot%d" % ((e + 2) % 3), align_bytes=64)
-            move = nc.vector.tensor_copy if e == 0 else nc.scalar.copy
-            move(xg[e][:], picked[e][:].rearrange("p u c -> p c u"))
+            nc.scalar.copy(
+                xg[e][:].rearrange("p (c i) u -> p c u i", i=2),
+                picked[e][:].rearrange("p u (c i) -> p c u i", i=2),
+            )
 
         def quantize_x(e):
             width = T if e == E else C
@@ -149,7 +153,11 @@ def tile_moe_shr_mlp_relu_kernel(
                         start=True,
                         stop=True,
                     )
-                nc.scalar.activation(hg[e][:, c0 : c0 + P, :], a[:].rearrange("p t c -> p c t"), RELU)
+                nc.scalar.activation(
+                    hg[e][:, c0 : c0 + P, :].rearrange("p (c i) t -> p c t i", i=2),
+                    a[:].rearrange("p t (c i) -> p c t i", i=2),
+                    RELU,
+                )
 
         def quantize_h(e):
             width = T if e == E else C
@@ -185,7 +193,7 @@ def tile_moe_shr_mlp_relu_kernel(
         nc.scalar.copy(xg[E][:], pairs[:].rearrange("p (u t) -> p t u", u=2))
 
 
-        permute(0)
+        permute(0, 2)
         gather_tokens(0)
         gather_tokens(1)
         weave(0)
@@ -195,7 +203,8 @@ def tile_moe_shr_mlp_relu_kernel(
             if e + 2 < E:
                 gather_tokens(e + 2)
             if e + 1 < E:
-                permute(e + 1)
+                if e % 2:
+                    permute(e + 1, e + 3)
                 weave(e + 1)
                 quantize_x(e + 1)
                 layer1(e + 1)
@@ -207,7 +216,7 @@ def tile_moe_shr_mlp_relu_kernel(
                 slots_results(0, e - 2, e, "wide")
             if e >= E - 2:
                 slots_results(0, e, e + 1, "first")
-        permute(E)
+        permute(E, E + 1)
         quantize_x(E)
 
         def product(b, r):

@@ -128,7 +128,8 @@ def tile_moe_shr_mlp_relu_kernel(
 
         def weave(e):
             xg[e] = keep.tile([P, C, 2], U32, name="xg%d" % e, tag="slot%d" % ((e + 2) % 3), align_bytes=64)
-            nc.scalar.copy(
+            move = nc.vector.tensor_copy if e == E - 1 else nc.scalar.copy
+            move(
                 xg[e][:].rearrange("p (c i) u -> p c u i", i=2),
                 picked[e][:].rearrange("p u (c i) -> p c u i", i=2),
             )
@@ -153,11 +154,12 @@ def tile_moe_shr_mlp_relu_kernel(
                         start=True,
                         stop=True,
                     )
-                nc.scalar.activation(
-                    hg[e][:, c0 : c0 + P, :].rearrange("p (c i) t -> p c t i", i=2),
-                    a[:].rearrange("p t (c i) -> p c t i", i=2),
-                    RELU,
-                )
+                hidden = hg[e][:, c0 : c0 + P, :].rearrange("p (c i) t -> p c t i", i=2)
+                sums = a[:].rearrange("p t (c i) -> p c t i", i=2)
+                if e == E - 1 and c0 > 0:
+                    nc.vector.tensor_scalar_max(hidden, sums, 0.0)
+                else:
+                    nc.scalar.activation(hidden, sums, RELU)
 
         def quantize_h(e):
             width = T if e == E else C
@@ -271,13 +273,22 @@ def tile_moe_shr_mlp_relu_kernel(
             shared_results(b)
         turn(turned0, [ys[0]], False, True)
         store_sum(0, turn_back(turned0))
-        prods2 = [product(2, r) for r in range(TOP)]
+        prods2 = [product(2, r) for r in range(TOP - 1)]
+        halves = [slice(c0, c0 + T // 2) for c0 in range(0, T, T // 2)]
+        last = []
+        for cols in halves:
+            prod = ring.tile([P, T // 2], F32, name="last")
+            offsets = pos_sb[TOP - 1][:, cols.start // 16 : cols.stop // 16]
+            nc.vector.tensor_tensor(prod[:], y[2][:].indirect(offsets), gate_sb[:, TOP - 1, cols], MULT)
+            last.append(prod)
         store_sum(1, add_up([ys[1]] + prods1))
         back = add_up([ys[2]] + prods2[:2])
-        partial = ring.tile([P, T], F32, name="partial")
-        nc.vector.tensor_tensor(partial[:], prods2[2][:], prods2[3][:], ADD)
-        for c0 in range(0, T, T // 2):
-            cols = slice(c0, c0 + T // 2)
-            result = ring.tile([P, T // 2], F32, name="last")
-            nc.vector.tensor_tensor(result[:], partial[:, cols], back[:, cols], ADD)
+        partial = []
+        for cols, prod in zip(halves, last):
+            both = ring.tile([P, T // 2], F32, name="both")
+            nc.vector.tensor_tensor(both[:], prods2[2][:, cols], prod[:], ADD)
+            partial.append(both)
+        for cols, both in zip(halves, partial):
+            result = ring.tile([P, T // 2], F32, name="final")
+            nc.vector.tensor_tensor(result[:], both[:], back[:, cols], ADD)
             nc.sync.dma_start(out[2 * P : 3 * P, cols], result[:])

@@ -240,7 +240,7 @@ def tile_moe_shr_mlp_relu_kernel(
                     )
 
         def add_up(terms):
-            turned = bank([P, T // P, P], "turned")
+            turned = bank([P, T // P, P], "first")
             turn(turned, terms, True, True)
             return turn_back(turned)
 

from contextlib import ExitStack

import concourse.mybir as mybir
from concourse.masks import make_identity

K, T, E, C, H, N = 512, 512, 8, 256, 512, 384
TOP = 4
S = E * C
FLOPS = 2 * (S + T) * (K * H + H * N)
BYTES = 4 * K * T + (E + 1) * (K * H + H * N) // 2 + (E + 1) * (K * H + H * N) // 32 + 4 * TOP * T + 4 * N * T

F32 = mybir.dt.float32
BF16 = mybir.dt.bfloat16
I32 = mybir.dt.int32
U32 = mybir.dt.uint32
U16 = mybir.dt.uint16
U8 = mybir.dt.uint8
FP8X4 = mybir.dt.float8_e4m3fn_x4
FP4X4 = mybir.dt.float4_e2m1fn_x4
RELU = mybir.ActivationFunctionType.Relu
MULT = mybir.AluOpType.mult
ADD = mybir.AluOpType.add

P = 128
PACK = 4
NB = N // P
PSUM_BUFS = {"wide": 3, "first": 2, "later": 2, "turned": 1}
W1_GROUPS = ((0, 4), (4, 9))


def tile_moe_shr_mlp_relu_kernel(
    tc, xT, w1_words, w1_scales, w2_words, w2_scales, gate, offs, pos1, pos2, pos3, pos4, out
):
    nc = tc.nc
    with ExitStack() as ctx:
        keep = ctx.enter_context(tc.tile_pool(name="keep", bufs=1))
        ring = ctx.enter_context(tc.tile_pool(name="ring", bufs=2))
        psum = ctx.enter_context(tc.psum_pool(name="psum", bufs=1))

        def bank(shape, tag):
            return psum.tile(shape, F32, name=tag, bufs=PSUM_BUFS[tag])

        s1_raw = [keep.tile([P, e1 - e0, H], U8, name="s1_raw%d" % e0, align_bytes=64) for e0, e1 in W1_GROUPS]
        nc.gpsimd.memset(s1_raw[0][:].bitcast(I32), 0)
        ident_raw = keep.tile([P, P], F32, name="ident_raw")
        make_identity(nc, ident_raw[:])
        ident = keep.tile([P, P], F32, name="ident")
        nc.scalar.activation(ident[:], ident_raw[:], RELU)

        s2 = keep.tile([P, E + 1, N], U8, name="s2", align_bytes=64)
        nc.vector.memset(s1_raw[1][:].bitcast(I32), 0)
        nc.vector.memset(s2[:].bitcast(I32), 0)

        def load_words(words, e0, e1, name, tag):
            t = keep.tile([P, e1 - e0, words.shape[3]], U8, name=name, tag=tag, align_bytes=64)
            nc.sync.dma_start(t[:].bitcast(I32), words[e0:e1, 0].rearrange("e p b -> p e b").bitcast(I32))
            return t

        def load_scales(plane, scales):
            rows = scales[:, 0].rearrange("e (q r) b -> r q e b", r=4)
            for r in range(4):
                nc.sync.dma_start(plane[r:P:32, :, :].bitcast(I32), rows[r].bitcast(I32))

        def load_list(lst, name):
            t = keep.tile([P, lst.shape[1]], U16, name=name)
            nc.sync.dma_start(t[:], lst)
            return t

        x_rows = xT.rearrange("(p u j) t -> u p j t", u=2, j=2)
        w1_raw = [load_words(w1_words, 0, 4, "w1_raw0", "w1_raw0")]
        load_scales(s1_raw[0], w1_scales[0:4])
        x_raw = []
        for u in range(2):
            t = keep.tile([P, 2, T], F32, name="x_raw%d" % u, tag="x_raw%d" % u, align_bytes=64)
            nc.sync.dma_start(t[:], x_rows[u])
            x_raw.append(t)
        offs_sb = load_list(offs, "offs_sb")
        pos_sb = [load_list(lst, "pos_sb%d" % r) for r, lst in enumerate((pos1, pos2, pos3, pos4))]
        load_scales(s1_raw[1], w1_scales[4:9])

        pairs = keep.tile([P, 2 * T], U32, name="pairs", tag="pairs", align_bytes=64)
        for u in range(2):
            nc.scalar.copy(
                pairs[:, u * T : (u + 1) * T].bitcast(BF16).rearrange("p (t j) -> p t j", j=2),
                x_raw[u][:].rearrange("p j t -> p t j"),
            )

        w1_raw.append(load_words(w1_words, 4, 9, "w1_raw1", "x_raw0"))
        w2 = load_words(w2_words, 0, E + 1, "w2", "x_raw1")
        load_scales(s2, w2_scales)

        w1 = {}
        s1 = {}

        def permute(e0, e1):
            g = 0 if e0 < 4 else 1
            held = slice(e0 - W1_GROUPS[g][0], e1 - W1_GROUPS[g][0])
            words = ring.tile([P, e1 - e0, 2 * H], U8, name="w1", align_bytes=64, bufs=2)
            nc.vector.tensor_copy(
                words[:].bitcast(U16).rearrange("p e (t a b) -> p e a t b", t=PACK, b=8),
                w1_raw[g][:, held, :].bitcast(U16).rearrange("p e (a b t) -> p e a t b", t=PACK, b=8),
            )
            scales = ring.tile([P, e1 - e0, H], U8, name="s1", align_bytes=64, bufs=2)
            nc.vector.tensor_copy(
                scales[:].rearrange("p e (t a b) -> p e a t b", t=PACK, b=16),
                s1_raw[g][:, held, :].rearrange("p e (a b t) -> p e a t b", t=PACK, b=16),
            )
            for e in range(e0, e1):
                w1[e] = words[:, e - e0, :]
                s1[e] = scales[:, e - e0, :]

        def quantize(grouped, width, name, tag):
            codes = keep.tile([P, width], U32, name=name + "_codes", tag=tag, align_bytes=64)
            scales = keep.tile([P, width], U8, name=name + "_scales", align_bytes=64)
            nc.vector.quantize_mx(out=codes[:].bitcast(FP8X4), scales=scales[:], in_=grouped)
            return codes, scales

        picked = {}
        xg = {}
        xq = {}
        hg = {}
        hq = {}

        def gather_tokens(e):
            picked[e] = keep.tile([P, 2, C], U32, name="picked%d" % e, tag="slot%d" % (e % 3), align_bytes=64)
            for u in range(2):
                nc.vector.tensor_copy(picked[e][:, u, :], pairs[:, u * T : (u + 1) * T].indirect(offs_sb[:, 16 * e : 16 * (e + 1)]))

        def weave(e):
            xg[e] = keep.tile([P, C, 2], U32, name="xg%d" % e, tag="slot%d" % ((e + 2) % 3), align_bytes=64)
            move = nc.vector.tensor_copy if e == E - 1 else nc.scalar.copy
            move(
                xg[e][:].rearrange("p (c i) u -> p c u i", i=2),
                picked[e][:].rearrange("p u (c i) -> p c u i", i=2),
            )

        def quantize_x(e):
            width = T if e == E else C
            xq[e] = quantize(xg[e][:].rearrange("p c u -> p (c u)").bitcast(BF16), width, "xq%d" % e, "hg7" if e == E else "xq%d" % e)

        def layer1(e):
            width = T if e == E else C
            codes, scales = xq[e]
            hg[e] = keep.tile([P, width, PACK], BF16, name="hg%d" % e, tag="hg%d" % e, align_bytes=64)
            for c0 in range(0, width, P):
                a = bank([P, PACK, P], "first" if e == E else "wide")
                for t in range(PACK):
                    nc.tensor.matmul_mx(
                        out=a[:, t, :],
                        lhsT=w1[e][:, 2 * P * t : 2 * P * (t + 1)].bitcast(FP4X4),
                        lhsT_scale=s1[e][:, P * t : P * (t + 1)],
                        rhs=codes[:, c0 : c0 + P].bitcast(FP8X4),
                        rhs_scale=scales[:, c0 : c0 + P],
                        start=True,
                        stop=True,
                    )
                hidden = hg[e][:, c0 : c0 + P, :].rearrange("p (c i) t -> p c t i", i=2)
                sums = a[:].rearrange("p t (c i) -> p c t i", i=2)
                if e == E - 1 and c0 > 0:
                    nc.vector.tensor_scalar_max(hidden, sums, 0.0)
                else:
                    nc.scalar.activation(hidden, sums, RELU)

        def quantize_h(e):
            width = T if e == E else C
            hq[e] = quantize(hg[e][:].rearrange("p c t -> p (c t)"), width, "hq%d" % e, "prod0_2" if e == E else "hq%d" % e)

        def layer2(e, b, dst):
            codes, scales = hq[e]
            nc.tensor.matmul_mx(
                out=dst,
                lhsT=w2[:, e, 2 * P * b : 2 * P * (b + 1)].bitcast(FP4X4),
                lhsT_scale=s2[:, e, P * b : P * (b + 1)],
                rhs=codes[:].bitcast(FP8X4),
                rhs_scale=scales[:],
                start=True,
                stop=True,
            )

        y = {0: keep.tile([P, S], F32, name="y0")}
        ys = [keep.tile([P, T], F32, name="ys%d" % b) for b in range(NB)]

        def slots_results(b, e0, e1, tag):
            acc = bank([P, (e1 - e0) * C], tag)
            for e in range(e0, e1):
                layer2(e, b, acc[:, (e - e0) * C : (e - e0 + 1) * C])
            nc.scalar.copy(y[b][:, e0 * C : e1 * C], acc[:])

        def shared_results(b):
            acc = bank([P, T], "later")
            layer2(E, b, acc[:])
            nc.scalar.copy(ys[b][:], acc[:])

        xg[E] = keep.tile([P, T, 2], U32, name="xg_shared", align_bytes=64)
        nc.scalar.copy(xg[E][:], pairs[:].rearrange("p (u t) -> p t u", u=2))


        permute(0, 2)
        gather_tokens(0)
        gather_tokens(1)
        weave(0)
        quantize_x(0)
        layer1(0)
        for e in range(E):
            if e + 2 < E:
                gather_tokens(e + 2)
            if e + 1 < E:
                if e % 2:
                    permute(e + 1, e + 3)
                weave(e + 1)
                quantize_x(e + 1)
                layer1(e + 1)
            if e == 2:
                gate_sb = keep.tile([P, TOP, T], F32, name="gate_sb", tag="w1_raw0", align_bytes=64)
                nc.sync.dma_start(gate_sb[:], gate[:, 0:P, :].rearrange("r p t -> p r t"))
            quantize_h(e)
            if e >= 2 and e % 2 == 0:
                slots_results(0, e - 2, e, "wide")
            if e >= E - 2:
                slots_results(0, e, e + 1, "first")
        permute(E, E + 1)
        quantize_x(E)

        def product(b, r):
            tag = "hg%d" % E if (b, r) == (1, 0) else "prod%d_%d" % (b, r)
            prod = keep.tile([P, T], F32, name="prod", tag=tag, align_bytes=64)
            nc.vector.tensor_tensor(prod[:], y[b][:].indirect(pos_sb[r][:]), gate_sb[:, r, :], MULT)
            return prod

        def turn(turned, terms, opens, closes):
            for i, term in enumerate(terms):
                for j in range(T // P):
                    nc.tensor.matmul(
                        turned[:, j, :],
                        term[:, j * P : (j + 1) * P],
                        ident[:],
                        start=(opens and i == 0 and j == 0),
                        stop=(closes and i == len(terms) - 1 and j == T // P - 1),
                        is_transpose=True,
                    )

        def add_up(terms):
            turned = bank([P, T // P, P], "first")
            turn(turned, terms, True, True)
            return turn_back(turned)

        def turn_back(turned):
            turned_sb = ring.tile([P, T // P, P], F32, name="turned_sb")
            nc.scalar.copy(turned_sb[:], turned[:])
            back = bank([P, T], "wide")
            for j in range(T // P):
                nc.tensor.transpose(back[:, j * P : (j + 1) * P], turned_sb[:, j, :], ident[:])
            return back

        def store_sum(b, back):
            result = ring.tile([P, T], F32, name="result")
            nc.scalar.copy(result[:], back[:])
            nc.sync.dma_start(out[b * P : (b + 1) * P, :], result[:])

        prods0 = [product(0, r) for r in range(TOP)]
        layer1(E)
        y[1] = keep.tile([P, S], F32, name="y1", tag="hg6", align_bytes=64)
        for e0 in range(0, E, 2):
            slots_results(1, e0, e0 + 2, "later" if e0 < E // 2 else "wide")
        turned0 = bank([P, T // P, P], "turned")
        turn(turned0, prods0, True, False)
        quantize_h(E)
        prods1 = [product(1, r) for r in range(TOP)]
        y[2] = keep.tile([P, S], F32, name="y2", tag="hg7", align_bytes=64)
        for e0 in range(0, E, 2):
            slots_results(2, e0, e0 + 2, "later" if e0 < E // 2 else "wide")
        for b in range(NB):
            shared_results(b)
        turn(turned0, [ys[0]], False, True)
        store_sum(0, turn_back(turned0))
        prods2 = [product(2, r) for r in range(TOP - 1)]
        halves = [slice(c0, c0 + T // 2) for c0 in range(0, T, T // 2)]
        last = []
        for cols in halves:
            prod = ring.tile([P, T // 2], F32, name="last")
            offsets = pos_sb[TOP - 1][:, cols.start // 16 : cols.stop // 16]
            nc.vector.tensor_tensor(prod[:], y[2][:].indirect(offsets), gate_sb[:, TOP - 1, cols], MULT)
            last.append(prod)
        store_sum(1, add_up([ys[1]] + prods1))
        back = add_up([ys[2]] + prods2[:2])
        partial = []
        for cols, prod in zip(halves, last):
            both = ring.tile([P, T // 2], F32, name="both")
            nc.vector.tensor_tensor(both[:], prods2[2][:, cols], prod[:], ADD)
            partial.append(both)
        for cols, both in zip(halves, partial):
            result = ring.tile([P, T // 2], F32, name="final")
            nc.vector.tensor_tensor(result[:], both[:], back[:, cols], ADD)
            nc.sync.dma_start(out[2 * P : 3 * P, cols], result[:])
